import numpy as np
import ml_dtypes


def mxq(x, axis, fmt="e4m3"):
    dtype, down = {"e4m3": (ml_dtypes.float8_e4m3fn, 7), "e5m2": (ml_dtypes.float8_e5m2, 14)}[fmt]
    v = np.moveaxis(np.asarray(x, np.float32).astype(ml_dtypes.bfloat16).astype(np.float64), axis, -1)
    blocks = v.reshape(v.shape[:-1] + (-1, 32))
    amax = np.abs(blocks).max(-1, keepdims=True)
    byte = np.maximum(np.where(amax > 0, np.frexp(amax)[1] - 1 + 127, 0) - down, 1)
    scale = np.exp2(byte - 127.0)
    codes = (blocks / scale).astype(np.float32).astype(dtype).astype(np.float64)
    return np.moveaxis((codes * scale).reshape(v.shape), -1, axis)


WIDE = False


def mx_kscale(k):
    if not WIDE:
        return np.ones(k)
    levels = np.array([10, -10, 5, -5, 0])
    if k % 512:
        return np.exp2(np.random.permutation(np.resize(levels, k // 32))).repeat(32)
    a = np.empty((k // 512, 16))
    for p in range(k // 512):
        a[p, :8] = np.random.permutation(np.resize(levels, 8))
        for g in range(8):
            far = levels[np.abs(levels - a[p, g]) >= 10]
            a[p, g + 8] = far[np.random.randint(len(far))]
    return np.exp2(a.ravel()).repeat(32)


def f64(x):
    return np.asarray(x).astype(np.float64)


def striped(idx):
    return np.tile(idx.reshape(-1, 16).T, (8, 1)).astype(np.uint16)


def unstriped(offs):
    return offs[:16].T.reshape(-1).astype(np.int64)


def relu(v):
    return np.maximum(v, 0.0)


K, T, E, C, H, N = 2560, 512, 2, 256, 512, 128


def by_expert(wq, xq):
    return np.concatenate([wq[e].T @ xq[:, e * C:(e + 1) * C] for e in range(E)], axis=1)


def setup_inputs():
    n = np.random.standard_normal
    s = mx_kscale(K)[:, None]
    u = mx_kscale(H)
    return {
        "xT": (n((K, T)) * s).astype(np.float32),
        "w1": (n((E, K, H)) / np.sqrt(K) / s[None] * u[None, None, :]).astype(np.float32),
        "w2": (n((E, H, N)) / np.sqrt(H) / u[None, :, None]).astype(np.float32),
        "gate": np.tile(np.random.uniform(0.2, 1.0, E * C), (N, 1)).astype(np.float32),
        "offs": striped(np.random.permutation(T)[:E * C]),
    }


def reference(xT, w1, w2, gate, offs):
    idx = unstriped(offs)
    xq = mxq(f64(xT)[:, idx], 0, "e4m3")
    h = relu(by_expert(mxq(f64(w1), 1, "e4m3"), xq))
    y = by_expert(mxq(f64(w2), 1, "e4m3"), mxq(h, 0, "e4m3"))
    out = np.zeros((N, T))
    out[:, idx] = f64(gate) * y
    return out

@@ -1,0 +1,227 @@
+import concourse.mybir as mybir
+
+K, T, E, C, H, N = 2560, 512, 2, 256, 512, 128
+FLOPS = 2 * E * C * (K * H + H * N)
+
+F32 = mybir.dt.float32
+BF16 = mybir.dt.bfloat16
+U32 = mybir.dt.uint32
+U16 = mybir.dt.uint16
+U8 = mybir.dt.uint8
+FP8X4 = mybir.dt.float8_e4m3fn_x4
+RELU = mybir.ActivationFunctionType.Relu
+MULT = mybir.AluOpType.mult
+MAX = mybir.AluOpType.max
+
+P = 128
+PACK = 4
+K_PASS = P * PACK
+PASSES = K // K_PASS
+HALF = C // 2
+X_CUT = 64
+LAST = (E - 1, PASSES - 1)
+L_CUT = 40
+W_CUT = 64
+
+
+def tile_routed_moe_kernel(tc, xT, w1, w2, gate, offs, out):
+    nc = tc.nc
+    with (
+        tc.tile_pool(name="keep", bufs=1) as keep,
+        tc.tile_pool(name="stage", bufs=4) as stage,
+        tc.psum_pool(name="psum", bufs=1) as psum,
+    ):
+        offsets = keep.tile([P, T // 16], U16, name="offsets")
+        nc.sync.dma_start(offsets[:], offs)
+        slots = [offsets[:, e * (C // 16) : (e + 1) * (C // 16)] for e in range(E)]
+
+        xv = xT.rearrange("(a p j) t -> a p j t", p=P, j=PACK)
+        wv = w1.rearrange("e (a p j) h -> e a p j h", p=P, j=PACK)
+        w2v = w2.rearrange("e (p j) n -> e p j n", j=PACK)
+        x_raw = [keep.tile([P, PACK, T], F32, name=f"x_raw{a}") for a in range(PASSES)]
+        w_raw = [[keep.tile([P, PACK, H], F32, name=f"w_raw{e}_{a}") for a in range(PASSES) if (e, a) != LAST] for e in range(E)]
+        last_raw = [keep.tile([P, PACK, H // 2], F32, name=f"last_raw{h}") for h in range(2)]
+        w2_raw = [keep.tile([P, PACK, N], F32, name=f"w2_raw{e}") for e in range(E)]
+        gates = [keep.tile([P, C], F32, name=f"gate{e}") for e in range(E)]
+        for a in range(PASSES):
+            nc.sync.dma_start(x_raw[a][:], xv[a])
+        for e in range(E):
+            for a in range(PASSES):
+                if (e, a) == LAST:
+                    for h in range(2):
+                        nc.sync.dma_start(last_raw[h][:], wv[e, a][:, :, h * H // 2 : (h + 1) * H // 2])
+                else:
+                    nc.sync.dma_start(w_raw[e][a][:], wv[e, a])
+            nc.sync.dma_start(w2_raw[e][:], w2v[e])
+            nc.sync.dma_start(gates[e][:], gate[:, e * C : (e + 1) * C])
+
+        x_codes = [keep.tile([P, T], U32, name=f"x_codes{a}", align_bytes=64) for a in range(PASSES)]
+        x_scales = [keep.tile([P, T], U8, name=f"x_scales{s}", align_bytes=64) for s in range(2)]
+        g_codes = [keep.tile([P, T], U32, name=f"g_codes{a}", align_bytes=64) for a in range(PASSES)]
+        g_scales = [keep.tile([P, T], U8, name=f"g_scales{s}", align_bytes=64) for s in range(2)]
+        for s in range(2):
+            nc.gpsimd.memset(x_scales[s][:], 0)
+
+        def copy_x(a):
+            grouped = stage.tile([P, T, PACK], BF16, name="x_grouped", align_bytes=64)
+            for eng, c0, c1 in ((nc.vector.tensor_copy, 0, X_CUT), (nc.scalar.copy, X_CUT, T)):
+                eng(
+                    grouped[:, c0:c1, :].rearrange("p (c i) j -> p c j i", i=4),
+                    x_raw[a][:, :, c0:c1].rearrange("p j (c i) -> p c j i", i=4),
+                )
+            return grouped
+
+        def quantize_x(a, grouped):
+            nc.vector.quantize_mx(
+                out=x_codes[a][:].bitcast(FP8X4),
+                scales=x_scales[a // 4][4 * (a % 4) : P, :],
+                in_=grouped[:].rearrange("p t j -> p (t j)"),
+            )
+
+        def gather_words(a, e):
+            nc.vector.tensor_copy(g_codes[a][:, e * C : (e + 1) * C], x_codes[a][:].indirect(slots[e]))
+
+        def gather_scales(s, e):
+            nc.vector.tensor_copy(g_scales[s][:, e * C : (e + 1) * C], x_scales[s][:].indirect(slots[e]))
+
+        w_codes = [[keep.tile([P, H], U32, name=f"w_codes{e}_{a}", align_bytes=64) for a in range(PASSES)] for e in range(E)]
+        w_scales = [[keep.tile([P, H], U8, name=f"w_scales{e}_{a}", align_bytes=64) for a in range(PASSES)] for e in range(E)]
+        w2_codes = [keep.tile([P, N], U32, name=f"w2_codes{e}", align_bytes=64) for e in range(E)]
+        w2_scales = [keep.tile([P, N], U8, name=f"w2_scales{e}", align_bytes=64) for e in range(E)]
+
+        def copy_w(e, a):
+            grouped = stage.tile([P, PACK, P, PACK], BF16, name="w_grouped", align_bytes=64)
+            for eng, m0, m1 in ((nc.vector.tensor_copy, 0, W_CUT), (nc.scalar.copy, W_CUT, P)):
+                eng(
+                    grouped[:, :, m0:m1, :].rearrange("p t m j -> p m j t"),
+                    w_raw[e][a][:, :, 4 * m0 : 4 * m1].rearrange("p j (m t) -> p m j t", t=4),
+                )
+            return grouped
+
+        def quantize_w(e, a, grouped):
+            nc.vector.quantize_mx(
+                out=w_codes[e][a][:].bitcast(FP8X4),
+                scales=w_scales[e][a][:],
+                in_=grouped[:].rearrange("p t m j -> p (t m j)"),
+            )
+
+        def copy_last(h):
+            grouped = stage.tile([P, PACK, P // 2, PACK], BF16, name="last_grouped", align_bytes=64)
+            for eng, m0, m1 in ((nc.vector.tensor_copy, 0, L_CUT), (nc.scalar.copy, L_CUT, P // 2)):
+                eng(
+                    grouped[:, :, m0:m1, :].rearrange("p t m j -> p m j t"),
+                    last_raw[h][:, :, 4 * m0 : 4 * m1].rearrange("p j (m t) -> p m j t", t=4),
+                )
+            return grouped
+
+        def quantize_last(h, grouped):
+            e, a = LAST
+            for t in range(PACK):
+                cols = slice(t * P + h * P // 2, t * P + (h + 1) * P // 2)
+                nc.vector.quantize_mx(
+                    out=w_codes[e][a][:, cols].bitcast(FP8X4),
+                    scales=w_scales[e][a][:, cols],
+                    in_=grouped[:, t, :, :].rearrange("p m j -> p (m j)"),
+                )
+
+        def prepare_w2(e):
+            grouped = stage.tile([P, N, PACK], BF16, name="w2_grouped", align_bytes=64)
+            nc.scalar.copy(
+                grouped[:].rearrange("p (c i) j -> p c j i", i=4),
+                w2_raw[e][:].rearrange("p j (c i) -> p c j i", i=4),
+            )
+            nc.vector.quantize_mx(
+                out=w2_codes[e][:].bitcast(FP8X4),
+                scales=w2_scales[e][:],
+                in_=grouped[:].rearrange("p n j -> p (n j)"),
+            )
+
+        banks = [[psum.tile([P, C], F32, name=f"bank{e}_{t}") for t in range(PACK)] for e in range(E)]
+
+        def multiply(e, a):
+            cols = slice(e * C, (e + 1) * C)
+            for t in range(PACK):
+                nc.tensor.matmul_mx(
+                    out=banks[e][t][:],
+                    lhsT=w_codes[e][a][:, t * P : (t + 1) * P].bitcast(FP8X4),
+                    lhsT_scale=w_scales[e][a][:, t * P : (t + 1) * P],
+                    rhs=g_codes[a][:, cols].bitcast(FP8X4),
+                    rhs_scale=g_scales[a // 4][4 * (a % 4) : P, cols],
+                    start=(a == 0),
+                    stop=(a == PASSES - 1),
+                )
+
+        placed = keep.tile([P, T], F32, name="placed")
+
+        def finish(e):
+            planes = keep.tile([P, PACK, C], BF16, name=f"planes{e}")
+            for t in range(PACK):
+                if t % 2 == 0 or e == 0:
+                    nc.scalar.activation(planes[:, t, :], banks[e][t][:], RELU)
+                else:
+                    nc.vector.tensor_scalar(planes[:, t, :], banks[e][t][:], 0.0, None, MAX)
+            h_codes = keep.tile([P, C], U32, name=f"h_codes{e}", align_bytes=64)
+            h_scales = keep.tile([P, C], U8, name=f"h_scales{e}", align_bytes=64)
+            grouped = keep.tile([P, C, PACK], BF16, name=f"h_grouped{e}", align_bytes=64)
+            for half in range(2):
+                c0 = half * HALF
+                eng = nc.vector.tensor_copy if half == 0 else nc.scalar.copy
+                eng(
+                    grouped[:, c0 : c0 + HALF, :].rearrange("p (c i) j -> p c j i", i=4),
+                    planes[:, :, c0 : c0 + HALF].rearrange("p j (c i) -> p c j i", i=4),
+                )
+            for half in range(2):
+                cols = slice(half * HALF, (half + 1) * HALF)
+                nc.vector.quantize_mx(
+                    out=h_codes[:, cols].bitcast(FP8X4),
+                    scales=h_scales[:, cols],
+                    in_=grouped[:, cols, :].rearrange("p c j -> p (c j)"),
+                )
+                y = psum.tile([P, HALF], F32, name=f"bank0_{2 * e + half}")
+                nc.tensor.matmul_mx(
+                    out=y[:],
+                    lhsT=w2_codes[e][:].bitcast(FP8X4),
+                    lhsT_scale=w2_scales[e][:],
+                    rhs=h_codes[:, cols].bitcast(FP8X4),
+                    rhs_scale=h_scales[:, cols],
+                    start=True,
+                    stop=True,
+                )
+                y_sb = keep.tile([P, HALF], F32, name=f"y_sb{e}_{half}")
+                nc.scalar.copy(y_sb[:], y[:])
+                o0 = (e * C + half * HALF) // 16
+                nc.vector.tensor_tensor(
+                    placed[:].indirect(offsets[:, o0 : o0 + HALF // 16]), y_sb[:], gates[e][:, cols], MULT
+                )
+
+        xg = copy_x(0)
+        for a in range(PASSES):
+            nxt = copy_x(a + 1) if a + 1 < PASSES else copy_w(0, 0)
+            quantize_x(a, xg)
+            gather_words(a, 0)
+            if a == 3:
+                gather_scales(0, 0)
+            xg = nxt
+        gather_scales(1, 0)
+
+        wg = xg
+        steps = [(e, a) for e in range(E) for a in range(PASSES)]
+        for i, (e, a) in enumerate(steps):
+            nxt = copy_w(*steps[i + 1]) if i + 2 < len(steps) else None
+            if (e, a) == LAST:
+                for h in range(2):
+                    quantize_last(h, copy_last(h))
+            else:
+                quantize_w(e, a, wg)
+            if e == 0:
+                gather_words(a, 1)
+                if a >= 3:
+                    gather_scales(a - 3, 1)
+            multiply(e, a)
+            if a == 3:
+                prepare_w2(e)
+            wg = nxt
+            if (e, a) == (1, 0):
+                finish(0)
+        finish(1)
+        nc.sync.dma_start(out, placed[:])

@@ -18,10 +18,10 @@ PACK = 4
 K_PASS = P * PACK
 PASSES = K // K_PASS
 HALF = C // 2
-X_CUT = 64
+X_CUT = 96
 LAST = (E - 1, PASSES - 1)
-L_CUT = 40
-W_CUT = 64
+F_CUT = 320
+T_CUT = 2
 
 
 def tile_routed_moe_kernel(tc, xT, w1, w2, gate, offs, out):
@@ -32,7 +32,6 @@ def tile_routed_moe_kernel(tc, xT, w1, w2, gate, offs, out):
         tc.psum_pool(name="psum", bufs=1) as psum,
     ):
         offsets = keep.tile([P, T // 16], U16, name="offsets")
-        nc.sync.dma_start(offsets[:], offs)
         slots = [offsets[:, e * (C // 16) : (e + 1) * (C // 16)] for e in range(E)]
 
         xv = xT.rearrange("(a p j) t -> a p j t", p=P, j=PACK)
@@ -40,16 +39,18 @@ def tile_routed_moe_kernel(tc, xT, w1, w2, gate, offs, out):
         w2v = w2.rearrange("e (p j) n -> e p j n", j=PACK)
         x_raw = [keep.tile([P, PACK, T], F32, name=f"x_raw{a}") for a in range(PASSES)]
         w_raw = [[keep.tile([P, PACK, H], F32, name=f"w_raw{e}_{a}") for a in range(PASSES) if (e, a) != LAST] for e in range(E)]
-        last_raw = [keep.tile([P, PACK, H // 2], F32, name=f"last_raw{h}") for h in range(2)]
+        last_raw = [keep.tile([P, 2, H], F32, name=f"last_raw{h}") for h in range(2)]
         w2_raw = [keep.tile([P, PACK, N], F32, name=f"w2_raw{e}") for e in range(E)]
         gates = [keep.tile([P, C], F32, name=f"gate{e}") for e in range(E)]
         for a in range(PASSES):
             nc.sync.dma_start(x_raw[a][:], xv[a])
+            if a == 0:
+                nc.sync.dma_start(offsets[:], offs)
         for e in range(E):
             for a in range(PASSES):
                 if (e, a) == LAST:
                     for h in range(2):
-                        nc.sync.dma_start(last_raw[h][:], wv[e, a][:, :, h * H // 2 : (h + 1) * H // 2])
+                        nc.sync.dma_start(last_raw[h][:], wv[e, a][:, 2 * h : 2 * h + 2, :])
                 else:
                     nc.sync.dma_start(w_raw[e][a][:], wv[e, a])
             nc.sync.dma_start(w2_raw[e][:], w2v[e])
@@ -64,7 +65,8 @@ def tile_routed_moe_kernel(tc, xT, w1, w2, gate, offs, out):
 
         def copy_x(a):
             grouped = stage.tile([P, T, PACK], BF16, name="x_grouped", align_bytes=64)
-            for eng, c0, c1 in ((nc.vector.tensor_copy, 0, X_CUT), (nc.scalar.copy, X_CUT, T)):
+            cut = F_CUT if a == 0 else X_CUT
+            for eng, c0, c1 in ((nc.vector.tensor_copy, 0, cut), (nc.scalar.copy, cut, T)):
                 eng(
                     grouped[:, c0:c1, :].rearrange("p (c i) j -> p c j i", i=4),
                     x_raw[a][:, :, c0:c1].rearrange("p j (c i) -> p c j i", i=4),
@@ -91,10 +93,10 @@ def tile_routed_moe_kernel(tc, xT, w1, w2, gate, offs, out):
 
         def copy_w(e, a):
             grouped = stage.tile([P, PACK, P, PACK], BF16, name="w_grouped", align_bytes=64)
-            for eng, m0, m1 in ((nc.vector.tensor_copy, 0, W_CUT), (nc.scalar.copy, W_CUT, P)):
+            for eng, t0, t1 in ((nc.vector.tensor_copy, 0, T_CUT), (nc.scalar.copy, T_CUT, PACK)):
                 eng(
-                    grouped[:, :, m0:m1, :].rearrange("p t m j -> p m j t"),
-                    w_raw[e][a][:, :, 4 * m0 : 4 * m1].rearrange("p j (m t) -> p m j t", t=4),
+                    grouped[:, t0:t1, :, :].rearrange("p t m j -> p m j t"),
+                    w_raw[e][a][:].rearrange("p j (m t) -> p m j t", t=4)[:, :, :, t0:t1],
                 )
             return grouped
 
@@ -105,27 +107,24 @@ def tile_routed_moe_kernel(tc, xT, w1, w2, gate, offs, out):
                 in_=grouped[:].rearrange("p t m j -> p (t m j)"),
             )
 
-        def copy_last(h):
-            grouped = stage.tile([P, PACK, P // 2, PACK], BF16, name="last_grouped", align_bytes=64)
-            for eng, m0, m1 in ((nc.vector.tensor_copy, 0, L_CUT), (nc.scalar.copy, L_CUT, P // 2)):
+        def copy_last(h, grouped):
+            for eng, t0, t1 in ((nc.vector.tensor_copy, 0, T_CUT), (nc.scalar.copy, T_CUT, PACK)):
                 eng(
-                    grouped[:, :, m0:m1, :].rearrange("p t m j -> p m j t"),
-                    last_raw[h][:, :, 4 * m0 : 4 * m1].rearrange("p j (m t) -> p m j t", t=4),
+                    grouped[:, t0:t1, :, 2 * h : 2 * h + 2].rearrange("p t m j -> p m j t"),
+                    last_raw[h][:].rearrange("p j (m t) -> p m j t", t=4)[:, :, :, t0:t1],
                 )
-            return grouped
 
-        def quantize_last(h, grouped):
+        def quantize_last(t, grouped):
             e, a = LAST
-            for t in range(PACK):
-                cols = slice(t * P + h * P // 2, t * P + (h + 1) * P // 2)
-                nc.vector.quantize_mx(
-                    out=w_codes[e][a][:, cols].bitcast(FP8X4),
-                    scales=w_scales[e][a][:, cols],
-                    in_=grouped[:, t, :, :].rearrange("p m j -> p (m j)"),
-                )
+            cols = slice(t * P, (t + 1) * P)
+            nc.vector.quantize_mx(
+                out=w_codes[e][a][:, cols].bitcast(FP8X4),
+                scales=w_scales[e][a][:, cols],
+                in_=grouped[:, t, :, :].rearrange("p m j -> p (m j)"),
+            )
 
         def prepare_w2(e):
-            grouped = stage.tile([P, N, PACK], BF16, name="w2_grouped", align_bytes=64)
+            grouped = stage.tile([P, N, PACK], BF16, name="w2_grouped", bufs=2, align_bytes=64)
             nc.scalar.copy(
                 grouped[:].rearrange("p (c i) j -> p c j i", i=4),
                 w2_raw[e][:].rearrange("p j (c i) -> p c j i", i=4),
@@ -209,8 +208,11 @@ def tile_routed_moe_kernel(tc, xT, w1, w2, gate, offs, out):
         for i, (e, a) in enumerate(steps):
             nxt = copy_w(*steps[i + 1]) if i + 2 < len(steps) else None
             if (e, a) == LAST:
+                grouped = stage.tile([P, PACK, P, PACK], BF16, name="w_grouped", align_bytes=64)
                 for h in range(2):
-                    quantize_last(h, copy_last(h))
+                    copy_last(h, grouped)
+                for t in range(PACK):
+                    quantize_last(t, grouped)
             else:
                 quantize_w(e, a, wg)
             if e == 0:

import concourse.mybir as mybir

K, T, E, C, H, N = 2560, 512, 2, 256, 512, 128
FLOPS = 2 * E * C * (K * H + H * N)

F32 = mybir.dt.float32
BF16 = mybir.dt.bfloat16
U32 = mybir.dt.uint32
U16 = mybir.dt.uint16
U8 = mybir.dt.uint8
FP8X4 = mybir.dt.float8_e4m3fn_x4
RELU = mybir.ActivationFunctionType.Relu
MULT = mybir.AluOpType.mult
MAX = mybir.AluOpType.max

P = 128
PACK = 4
K_PASS = P * PACK
PASSES = K // K_PASS
HALF = C // 2
X_CUT = 96
LAST = (E - 1, PASSES - 1)
F_CUT = 320
T_CUT = 2


def tile_routed_moe_kernel(tc, xT, w1, w2, gate, offs, out):
    nc = tc.nc
    with (
        tc.tile_pool(name="keep", bufs=1) as keep,
        tc.tile_pool(name="stage", bufs=4) as stage,
        tc.psum_pool(name="psum", bufs=1) as psum,
    ):
        offsets = keep.tile([P, T // 16], U16, name="offsets")
        slots = [offsets[:, e * (C // 16) : (e + 1) * (C // 16)] for e in range(E)]

        xv = xT.rearrange("(a p j) t -> a p j t", p=P, j=PACK)
        wv = w1.rearrange("e (a p j) h -> e a p j h", p=P, j=PACK)
        w2v = w2.rearrange("e (p j) n -> e p j n", j=PACK)
        x_raw = [keep.tile([P, PACK, T], F32, name=f"x_raw{a}") for a in range(PASSES)]
        w_raw = [[keep.tile([P, PACK, H], F32, name=f"w_raw{e}_{a}") for a in range(PASSES) if (e, a) != LAST] for e in range(E)]
        last_raw = [keep.tile([P, 2, H], F32, name=f"last_raw{h}") for h in range(2)]
        w2_raw = [keep.tile([P, PACK, N], F32, name=f"w2_raw{e}") for e in range(E)]
        gates = [keep.tile([P, C], F32, name=f"gate{e}") for e in range(E)]
        for a in range(PASSES):
            nc.sync.dma_start(x_raw[a][:], xv[a])
            if a == 0:
                nc.sync.dma_start(offsets[:], offs)
        for e in range(E):
            for a in range(PASSES):
                if (e, a) == LAST:
                    for h in range(2):
                        nc.sync.dma_start(last_raw[h][:], wv[e, a][:, 2 * h : 2 * h + 2, :])
                else:
                    nc.sync.dma_start(w_raw[e][a][:], wv[e, a])
            nc.sync.dma_start(w2_raw[e][:], w2v[e])
            nc.sync.dma_start(gates[e][:], gate[:, e * C : (e + 1) * C])

        x_codes = [keep.tile([P, T], U32, name=f"x_codes{a}", align_bytes=64) for a in range(PASSES)]
        x_scales = [keep.tile([P, T], U8, name=f"x_scales{s}", align_bytes=64) for s in range(2)]
        g_codes = [keep.tile([P, T], U32, name=f"g_codes{a}", align_bytes=64) for a in range(PASSES)]
        g_scales = [keep.tile([P, T], U8, name=f"g_scales{s}", align_bytes=64) for s in range(2)]
        for s in range(2):
            nc.gpsimd.memset(x_scales[s][:], 0)

        def copy_x(a):
            grouped = stage.tile([P, T, PACK], BF16, name="x_grouped", align_bytes=64)
            cut = F_CUT if a == 0 else X_CUT
            for eng, c0, c1 in ((nc.vector.tensor_copy, 0, cut), (nc.scalar.copy, cut, T)):
                eng(
                    grouped[:, c0:c1, :].rearrange("p (c i) j -> p c j i", i=4),
                    x_raw[a][:, :, c0:c1].rearrange("p j (c i) -> p c j i", i=4),
                )
            return grouped

        def quantize_x(a, grouped):
            nc.vector.quantize_mx(
                out=x_codes[a][:].bitcast(FP8X4),
                scales=x_scales[a // 4][4 * (a % 4) : P, :],
                in_=grouped[:].rearrange("p t j -> p (t j)"),
            )

        def gather_words(a, e):
            nc.vector.tensor_copy(g_codes[a][:, e * C : (e + 1) * C], x_codes[a][:].indirect(slots[e]))

        def gather_scales(s, e):
            nc.vector.tensor_copy(g_scales[s][:, e * C : (e + 1) * C], x_scales[s][:].indirect(slots[e]))

        w_codes = [[keep.tile([P, H], U32, name=f"w_codes{e}_{a}", align_bytes=64) for a in range(PASSES)] for e in range(E)]
        w_scales = [[keep.tile([P, H], U8, name=f"w_scales{e}_{a}", align_bytes=64) for a in range(PASSES)] for e in range(E)]
        w2_codes = [keep.tile([P, N], U32, name=f"w2_codes{e}", align_bytes=64) for e in range(E)]
        w2_scales = [keep.tile([P, N], U8, name=f"w2_scales{e}", align_bytes=64) for e in range(E)]

        def copy_w(e, a):
            grouped = stage.tile([P, PACK, P, PACK], BF16, name="w_grouped", align_bytes=64)
            for eng, t0, t1 in ((nc.vector.tensor_copy, 0, T_CUT), (nc.scalar.copy, T_CUT, PACK)):
                eng(
                    grouped[:, t0:t1, :, :].rearrange("p t m j -> p m j t"),
                    w_raw[e][a][:].rearrange("p j (m t) -> p m j t", t=4)[:, :, :, t0:t1],
                )
            return grouped

        def quantize_w(e, a, grouped):
            nc.vector.quantize_mx(
                out=w_codes[e][a][:].bitcast(FP8X4),
                scales=w_scales[e][a][:],
                in_=grouped[:].rearrange("p t m j -> p (t m j)"),
            )

        def copy_last(h, grouped):
            for eng, t0, t1 in ((nc.vector.tensor_copy, 0, T_CUT), (nc.scalar.copy, T_CUT, PACK)):
                eng(
                    grouped[:, t0:t1, :, 2 * h : 2 * h + 2].rearrange("p t m j -> p m j t"),
                    last_raw[h][:].rearrange("p j (m t) -> p m j t", t=4)[:, :, :, t0:t1],
                )

        def quantize_last(t, grouped):
            e, a = LAST
            cols = slice(t * P, (t + 1) * P)
            nc.vector.quantize_mx(
                out=w_codes[e][a][:, cols].bitcast(FP8X4),
                scales=w_scales[e][a][:, cols],
                in_=grouped[:, t, :, :].rearrange("p m j -> p (m j)"),
            )

        def prepare_w2(e):
            grouped = stage.tile([P, N, PACK], BF16, name="w2_grouped", bufs=2, align_bytes=64)
            nc.scalar.copy(
                grouped[:].rearrange("p (c i) j -> p c j i", i=4),
                w2_raw[e][:].rearrange("p j (c i) -> p c j i", i=4),
            )
            nc.vector.quantize_mx(
                out=w2_codes[e][:].bitcast(FP8X4),
                scales=w2_scales[e][:],
                in_=grouped[:].rearrange("p n j -> p (n j)"),
            )

        banks = [[psum.tile([P, C], F32, name=f"bank{e}_{t}") for t in range(PACK)] for e in range(E)]

        def multiply(e, a):
            cols = slice(e * C, (e + 1) * C)
            for t in range(PACK):
                nc.tensor.matmul_mx(
                    out=banks[e][t][:],
                    lhsT=w_codes[e][a][:, t * P : (t + 1) * P].bitcast(FP8X4),
                    lhsT_scale=w_scales[e][a][:, t * P : (t + 1) * P],
                    rhs=g_codes[a][:, cols].bitcast(FP8X4),
                    rhs_scale=g_scales[a // 4][4 * (a % 4) : P, cols],
                    start=(a == 0),
                    stop=(a == PASSES - 1),
                )

        placed = keep.tile([P, T], F32, name="placed")

        def finish(e):
            planes = keep.tile([P, PACK, C], BF16, name=f"planes{e}")
            for t in range(PACK):
                if t % 2 == 0 or e == 0:
                    nc.scalar.activation(planes[:, t, :], banks[e][t][:], RELU)
                else:
                    nc.vector.tensor_scalar(planes[:, t, :], banks[e][t][:], 0.0, None, MAX)
            h_codes = keep.tile([P, C], U32, name=f"h_codes{e}", align_bytes=64)
            h_scales = keep.tile([P, C], U8, name=f"h_scales{e}", align_bytes=64)
            grouped = keep.tile([P, C, PACK], BF16, name=f"h_grouped{e}", align_bytes=64)
            for half in range(2):
                c0 = half * HALF
                eng = nc.vector.tensor_copy if half == 0 else nc.scalar.copy
                eng(
                    grouped[:, c0 : c0 + HALF, :].rearrange("p (c i) j -> p c j i", i=4),
                    planes[:, :, c0 : c0 + HALF].rearrange("p j (c i) -> p c j i", i=4),
                )
            for half in range(2):
                cols = slice(half * HALF, (half + 1) * HALF)
                nc.vector.quantize_mx(
                    out=h_codes[:, cols].bitcast(FP8X4),
                    scales=h_scales[:, cols],
                    in_=grouped[:, cols, :].rearrange("p c j -> p (c j)"),
                )
                y = psum.tile([P, HALF], F32, name=f"bank0_{2 * e + half}")
                nc.tensor.matmul_mx(
                    out=y[:],
                    lhsT=w2_codes[e][:].bitcast(FP8X4),
                    lhsT_scale=w2_scales[e][:],
                    rhs=h_codes[:, cols].bitcast(FP8X4),
                    rhs_scale=h_scales[:, cols],
                    start=True,
                    stop=True,
                )
                y_sb = keep.tile([P, HALF], F32, name=f"y_sb{e}_{half}")
                nc.scalar.copy(y_sb[:], y[:])
                o0 = (e * C + half * HALF) // 16
                nc.vector.tensor_tensor(
                    placed[:].indirect(offsets[:, o0 : o0 + HALF // 16]), y_sb[:], gates[e][:, cols], MULT
                )

        xg = copy_x(0)
        for a in range(PASSES):
            nxt = copy_x(a + 1) if a + 1 < PASSES else copy_w(0, 0)
            quantize_x(a, xg)
            gather_words(a, 0)
            if a == 3:
                gather_scales(0, 0)
            xg = nxt
        gather_scales(1, 0)

        wg = xg
        steps = [(e, a) for e in range(E) for a in range(PASSES)]
        for i, (e, a) in enumerate(steps):
            nxt = copy_w(*steps[i + 1]) if i + 2 < len(steps) else None
            if (e, a) == LAST:
                grouped = stage.tile([P, PACK, P, PACK], BF16, name="w_grouped", align_bytes=64)
                for h in range(2):
                    copy_last(h, grouped)
                for t in range(PACK):
                    quantize_last(t, grouped)
            else:
                quantize_w(e, a, wg)
            if e == 0:
                gather_words(a, 1)
                if a >= 3:
                    gather_scales(a - 3, 1)
            multiply(e, a)
            if a == 3:
                prepare_w2(e)
            wg = nxt
            if (e, a) == (1, 0):
                finish(0)
        finish(1)
        nc.sync.dma_start(out, placed[:])
